import numpy as np
import ml_dtypes


def mxq(x, axis, fmt="e4m3"):
    dtype, down = {"e4m3": (ml_dtypes.float8_e4m3fn, 7), "e5m2": (ml_dtypes.float8_e5m2, 14)}[fmt]
    v = np.moveaxis(np.asarray(x, np.float32).astype(ml_dtypes.bfloat16).astype(np.float64), axis, -1)
    blocks = v.reshape(v.shape[:-1] + (-1, 32))
    amax = np.abs(blocks).max(-1, keepdims=True)
    byte = np.maximum(np.where(amax > 0, np.frexp(amax)[1] - 1 + 127, 0) - down, 1)
    scale = np.exp2(byte - 127.0)
    codes = (blocks / scale).astype(np.float32).astype(dtype).astype(np.float64)
    return np.moveaxis((codes * scale).reshape(v.shape), -1, axis)


WIDE = False


def mx_kscale(k):
    if not WIDE:
        return np.ones(k)
    levels = np.array([10, -10, 5, -5, 0])
    if k % 512:
        return np.exp2(np.random.permutation(np.resize(levels, k // 32))).repeat(32)
    a = np.empty((k // 512, 16))
    for p in range(k // 512):
        a[p, :8] = np.random.permutation(np.resize(levels, 8))
        for g in range(8):
            far = levels[np.abs(levels - a[p, g]) >= 10]
            a[p, g + 8] = far[np.random.randint(len(far))]
    return np.exp2(a.ravel()).repeat(32)


def f64(x):
    return np.asarray(x).astype(np.float64)


def striped(idx):
    return np.tile(idx.reshape(-1, 16).T, (8, 1)).astype(np.uint16)


def unstriped(offs):
    return offs[:16].T.reshape(-1).astype(np.int64)


def striped8(idx):
    return np.concatenate([x.reshape(-1, 16).T for x in idx]).astype(np.uint16)


def runs(offs, k):
    lists = np.stack([offs[16 * r : 16 * r + 16].T.reshape(-1) for r in range(8)]).astype(np.int64)
    return lists[np.arange(k) % 512 // 64]


def pack_weight(w):
    k, n = w.shape
    w = f64(np.asarray(w, np.float32).astype(ml_dtypes.bfloat16)).reshape(k // 32, 32, n)
    amax = np.abs(w).max(1)
    byte = np.clip(np.where(amax > 0, np.frexp(amax)[1] - 1 + 127 - 7, 1), 1, 254)
    scaled = (w * np.exp2(127.0 - byte)[:, None, :]).reshape(k, n).astype(np.float32)
    words = np.ascontiguousarray(scaled.reshape(k // 512, 128, 4, n).transpose(0, 1, 3, 2)).astype(ml_dtypes.float8_e4m3fn).view(np.uint8)
    return words, np.ascontiguousarray(byte.astype(np.uint8).reshape(k // 512, 16, n))


def unpack_weight(words, scales):
    g, p, n, _ = words.shape
    vals = np.ascontiguousarray(words).view(ml_dtypes.float8_e4m3fn).astype(np.float64) * np.repeat(np.exp2(scales.astype(np.float64) - 127.0), 8, axis=1)[..., None]
    return vals.transpose(0, 1, 3, 2).reshape(g * 512, n)


def sigmoid(v):
    return 1.0 / (1.0 + np.exp(-np.maximum(v, -700.0)))


K, T, S, V, H = 512, 2048, 512, 512, 512


def setup_inputs():
    n = np.random.standard_normal
    s = mx_kscale(K)[:, None]
    u = mx_kscale(S)
    packed_xT = pack_weight(n((K, T)) * s)
    return {
        "x_words": packed_xT[0],
        "x_scales": packed_xT[1],
        "w1": (n((K, H)) / np.sqrt(K) / s).astype(np.float32),
        "w2": (n((K, H)) / np.sqrt(K) / s).astype(np.float32),
        "ga": (np.random.uniform(0.5, 1.5, (H, 1)) * u[:, None]).astype(np.float32),
        "gb": (np.random.uniform(0.5, 1.5, (H, 1)) / u[:, None]).astype(np.float32),
        "offs": striped(np.random.permutation(T)[:S]),
        "two": striped(np.random.permutation(T)[:V]),
        "n1": striped8(np.stack([np.random.permutation(S) for _ in range(8)])),
        "n2": striped8(np.stack([np.random.permutation(S) for _ in range(8)])),
        "n3": striped8(np.stack([np.random.permutation(V) for _ in range(8)])),
        "n4": striped8(np.stack([np.random.permutation(V) for _ in range(8)])),
        "n5": striped8(np.stack([np.random.permutation(V) for _ in range(8)])),
        "n6": striped8(np.stack([np.random.permutation(V) for _ in range(8)])),
    }


def reference(x_words, x_scales, w1, w2, ga, gb, offs, two, n1, n2, n3, n4, n5, n6):
    xq = unpack_weight(x_words, x_scales)[:, unstriped(offs)]
    a = mxq(f64(w1), 0, "e4m3").T @ xq
    pa = a[np.arange(H)[:, None], runs(n1, H)]
    pb = a[np.arange(H)[:, None], runs(n2, H)]
    z = f64(ga) * (np.maximum(np.minimum(a, pa), np.minimum(np.maximum(a, pa), pb)))
    x_two = unpack_weight(x_words, x_scales)[:, unstriped(two)]
    b = mxq(f64(w2), 0, "e4m3").T @ x_two
    st = b[np.arange(H)[:, None], runs(n3, H)] - b
    z2 = f64(gb) * (b * (sigmoid(st[np.arange(H)[:, None], runs(n4, H)])))
    s = 0.0625 * ((mxq(z, 0, "e4m3").T @ mxq(z2, 0, "e4m3")))
    st2 = s + 0.5 * (s[np.arange(S)[:, None], runs(n5, S)])
    return st2 - (st2[np.arange(S)[:, None], runs(n6, S)])

@@ -1,0 +1,247 @@
+from contextlib import ExitStack
+
+import concourse.mybir as mybir
+
+K, T, S, V, H = 512, 2048, 512, 512, 512
+FLOPS = 2 * K * H * S + 2 * K * H * V + 2 * H * S * V
+
+F32 = mybir.dt.float32
+BF16 = mybir.dt.bfloat16
+I32 = mybir.dt.int32
+U32 = mybir.dt.uint32
+U16 = mybir.dt.uint16
+U8 = mybir.dt.uint8
+FP8X4 = mybir.dt.float8_e4m3fn_x4
+ALU = mybir.AluOpType
+ACT = mybir.ActivationFunctionType
+
+P = 128
+PACK = 4
+N = 512
+HALF = N // 2
+WINDOW = 2 * N
+
+
+def tile_picked_kqmedhopdhop_none_p_kernel(tc, x_words, x_scales, w1, w2, ga, gb, offs, two, n1, n2, n3, n4, n5, n6, out):
+    nc = tc.nc
+    with ExitStack() as ctx:
+        sb = ctx.enter_context(tc.tile_pool(name="sb", bufs=1))
+        psum = ctx.enter_context(tc.psum_pool(name="psum", bufs=1))
+
+        def load_list(src, name):
+            tile = sb.tile([P, N // 16], U16, name=name)
+            nc.sync.dma_start(tile[:], src)
+            return tile
+
+        def load_weight(src, name):
+            raw = sb.tile([P, PACK, N], F32, name=name)
+            nc.sync.dma_start(raw[:], src.rearrange("(p j) c -> p j c", j=PACK))
+            return raw
+
+        def load_gain(src, name):
+            tile = sb.tile([P, PACK], F32, name=name)
+            nc.sync.dma_start(tile[:], src.rearrange("(p t) o -> p (t o)", t=PACK))
+            return tile
+
+        def mx_pair(name):
+            codes = sb.tile([P, N], U32, name=name + "_codes", align_bytes=64)
+            scales = sb.tile([P, N], U8, name=name + "_scales", align_bytes=64)
+            return codes, scales
+
+        def staged(name):
+            return sb.tile([P, PACK * HALF], BF16, name=name, align_bytes=64)
+
+        def quantize(pair, h, src):
+            cols = slice(h * HALF, (h + 1) * HALF)
+            nc.vector.quantize_mx(out=pair[0][:, cols].bitcast(FP8X4), scales=pair[1][:, cols], in_=src[:])
+
+        def dealt_out(tile):
+            return tile[:].rearrange("p (e m k) -> p m k e", e=2, k=PACK)
+
+        def dealt_in(tile, h):
+            return tile[:].rearrange("p k (m t) -> p m k t", t=PACK)[:, :, :, 2 * h : 2 * h + 2]
+
+        def product(lhs, rhs, t, tag):
+            acc = psum.tile([P, N], F32, name=tag)
+            cols = slice(t * P, (t + 1) * P)
+            nc.tensor.matmul_mx(
+                out=acc[:],
+                lhsT=lhs[0][:, cols].bitcast(FP8X4),
+                lhsT_scale=lhs[1][:, cols],
+                rhs=rhs[0][:].bitcast(FP8X4),
+                rhs_scale=rhs[1][:],
+                start=True,
+                stop=True,
+            )
+            return acc
+
+        table_scales = sb.tile([P, T], U8, name="table_scales")
+        nc.vector.memset(table_scales[:].bitcast(I32), 0)
+        l_offs = load_list(offs, "l_offs")
+        w1_raw = load_weight(w1, "w1_raw")
+        for q in range(4):
+            nc.sync.dma_start(
+                table_scales[32 * q : 32 * q + 4, :].bitcast(I32), x_scales[0, 4 * q : 4 * q + 4, :].bitcast(I32)
+            )
+        table_words = sb.tile([P, T], I32, name="table_words")
+        nc.sync.dma_start(table_words[:], x_words[0].rearrange("p n t -> p (n t)").bitcast(I32))
+        l_two = load_list(two, "l_two")
+        ga_t = load_gain(ga, "ga_t")
+        l1 = load_list(n1, "l1")
+        l2 = load_list(n2, "l2")
+        w2_raw = load_weight(w2, "w2_raw")
+        gb_t = load_gain(gb, "gb_t")
+        l3 = load_list(n3, "l3")
+        l4 = load_list(n4, "l4")
+        l5 = load_list(n5, "l5")
+        l6 = load_list(n6, "l6")
+
+        xa = mx_pair("xa")
+        xb = mx_pair("xb")
+        w1q = mx_pair("w1q")
+        w1_bf = [staged("w1_bf0"), staged("w1_bf1")]
+        for h in range(2):
+            nc.scalar.copy(dealt_out(w1_bf[h]), dealt_in(w1_raw, h))
+        nc.vector.tensor_copy(xa[1][:], table_scales[:].indirect(l_offs[:]))
+        quantize(w1q, 0, w1_bf[0])
+        nc.vector.tensor_copy(xa[0][:], table_words[:].bitcast(U32).indirect(l_offs[:]))
+        quantize(w1q, 1, w1_bf[1])
+        nc.vector.tensor_copy(xb[1][:], table_scales[:].indirect(l_two[:]))
+        nc.vector.tensor_copy(xb[0][:], table_words[:].bitcast(U32).indirect(l_two[:]))
+
+        win_a = [sb.tile([P, WINDOW], F32, name=f"win_a{t}") for t in range(PACK)]
+        win_b = [sb.tile([P, WINDOW], F32, name=f"win_b{t}") for t in range(PACK)]
+        a_plain = sb.tile([P, PACK, N], F32, name="a_plain")
+        b_plain = sb.tile([P, PACK, N], F32, name="b_plain")
+        b_gain = sb.tile([P, PACK, N], F32, name="b_gain")
+        d1 = sb.tile([P, PACK, N], F32, name="d1")
+        d2 = sb.tile([P, PACK, N], F32, name="d2")
+        upper = sb.tile([P, PACK, N], F32, name="upper")
+        mid = sb.tile([P, PACK, N], F32, name="mid")
+        gate = sb.tile([P, PACK, N], F32, name="gate")
+        st = [sb.tile([P, N], F32, name=f"st{t}") for t in range(PACK)]
+
+        def project_a(t):
+            acc = product(w1q, xa, t, f"bank_a{t}")
+            nc.scalar.activation(win_a[t][:, :N], acc[:], ACT.Copy, scale=ga_t[:, t : t + 1])
+            nc.scalar.activation(a_plain[:, t, :], acc[:], ACT.Copy, scale=ga_t[:, t : t + 1])
+
+        def pulls(t):
+            nc.vector.tensor_tensor(d1[:, t, :], win_a[t][:].indirect(l1[:]), a_plain[:, t, :], ALU.subtract)
+            nc.vector.tensor_tensor(d2[:, t, :], win_a[t][:].indirect(l2[:]), a_plain[:, t, :], ALU.subtract)
+
+        def clip_above(h):
+            rows = slice(2 * h, 2 * h + 2)
+            nc.vector.scalar_tensor_tensor(upper[:, rows, :], d1[:, rows, :], 0.0, d2[:, rows, :], ALU.max, ALU.min)
+
+        def clip_below(h):
+            rows = slice(2 * h, 2 * h + 2)
+            nc.vector.scalar_tensor_tensor(mid[:, rows, :], d1[:, rows, :], 0.0, upper[:, rows, :], ALU.min, ALU.max)
+
+        b_acc = []
+
+        def project_b(t):
+            acc = product(w2q, xb, t, f"bank_b{t}")
+            b_acc.append(acc)
+            nc.scalar.copy(win_b[t][:, :N], acc[:])
+            nc.scalar.copy(b_plain[:, t, :], acc[:])
+
+        def step_b(t):
+            nc.vector.tensor_tensor(st[t][:], win_b[t][:].indirect(l3[:]), b_plain[:, t, :], ALU.subtract)
+
+        def gate_b(t):
+            for h in range(2):
+                nc.scalar.activation(
+                    gate[:, t, h * HALF : (h + 1) * HALF],
+                    st[t][:].indirect(l4[:, h * HALF // 16 : (h + 1) * HALF // 16]),
+                    ACT.Sigmoid,
+                )
+            nc.scalar.activation(b_gain[:, t, :], b_acc[t][:], ACT.Copy, scale=gb_t[:, t : t + 1])
+
+        project_a(0)
+        project_a(1)
+        w2q = mx_pair("w2q")
+        w2_bf = [staged("w2_bf0"), staged("w2_bf1")]
+        for h in range(2):
+            nc.scalar.copy(dealt_out(w2_bf[h]), dealt_in(w2_raw, h))
+        pulls(0)
+        pulls(1)
+        project_a(2)
+        project_a(3)
+        for h in range(2):
+            quantize(w2q, h, w2_bf[h])
+        clip_above(0)
+        project_b(0)
+        project_b(1)
+        pulls(2)
+        clip_below(0)
+        step_b(0)
+        step_b(1)
+        project_b(2)
+        project_b(3)
+        gate_b(0)
+        gate_b(1)
+        pulls(3)
+        step_b(2)
+        step_b(3)
+        gate_b(2)
+        gate_b(3)
+        clip_above(1)
+        clip_below(1)
+
+        zq = mx_pair("zq")
+        z2q = mx_pair("z2q")
+        z_bf = [staged("z_bf0"), staged("z_bf1")]
+        z2_bf = [staged("z2_bf0"), staged("z2_bf1")]
+
+        def finish_z2(h):
+            cols = slice(h * HALF, (h + 1) * HALF)
+            nc.vector.tensor_tensor(
+                z2_bf[h][:].rearrange("p (c i k) -> p c k i", i=4, k=PACK),
+                b_gain[:, :, cols].rearrange("p k (c i) -> p c k i", i=4),
+                gate[:, :, cols].rearrange("p k (c i) -> p c k i", i=4),
+                ALU.mult,
+            )
+
+        def finish_z(h):
+            nc.vector.tensor_tensor(dealt_out(z_bf[h]), dealt_in(mid, h), dealt_in(a_plain, h), ALU.add)
+
+        finish_z2(0)
+        finish_z2(1)
+        quantize(z2q, 0, z2_bf[0])
+        finish_z(0)
+        quantize(z2q, 1, z2_bf[1])
+        quantize(zq, 0, z_bf[0])
+        finish_z(1)
+        quantize(zq, 1, z_bf[1])
+
+        s_plain = [sb.tile([P, N], F32, name=f"s_plain{t}") for t in range(PACK)]
+        st2_plain = [sb.tile([P, N], F32, name=f"st2_plain{t}") for t in range(PACK)]
+        result = [sb.tile([P, N], F32, name=f"result{t}") for t in range(PACK)]
+        out_rows = out.rearrange("(p t) v -> p t v", t=PACK)
+
+        def scores(t):
+            acc = product(zq, z2q, t, f"bank_a{t}")
+            nc.scalar.activation(win_a[t][:, :N], acc[:], ACT.Copy, scale=-0.03125)
+            nc.scalar.activation(s_plain[t][:], acc[:], ACT.Copy, scale=-0.0625)
+
+        def first_hop(t):
+            nc.vector.tensor_tensor(win_b[t][:, :N], win_a[t][:].indirect(l5[:]), s_plain[t][:], ALU.add)
+            nc.scalar.copy(st2_plain[t][:], win_b[t][:, :N])
+
+        def second_hop(t):
+            nc.vector.tensor_tensor(result[t][:], win_b[t][:].indirect(l6[:]), st2_plain[t][:], ALU.subtract)
+            nc.sync.dma_start(out_rows[:, t, :], result[t][:])
+
+        scores(0)
+        scores(1)
+        first_hop(0)
+        scores(2)
+        first_hop(1)
+        scores(3)
+        second_hop(0)
+        first_hop(2)
+        second_hop(1)
+        first_hop(3)
+        second_hop(2)
+        second_hop(3)

@@ -20,12 +20,14 @@ PACK = 4
 N = 512
 HALF = N // 2
 WINDOW = 2 * N
+WEIGHT_AT = {"w1_raw": 0, "w2_raw": 8192}
 
 
 def tile_picked_kqmedhopdhop_none_p_kernel(tc, x_words, x_scales, w1, w2, ga, gb, offs, two, n1, n2, n3, n4, n5, n6, out):
     nc = tc.nc
     with ExitStack() as ctx:
         sb = ctx.enter_context(tc.tile_pool(name="sb", bufs=1))
+        shared = ctx.enter_context(tc.tile_pool(name="shared", bufs=1))
         psum = ctx.enter_context(tc.psum_pool(name="psum", bufs=1))
 
         def load_list(src, name):
@@ -34,7 +36,7 @@ def tile_picked_kqmedhopdhop_none_p_kernel(tc, x_words, x_scales, w1, w2, ga, gb
             return tile
 
         def load_weight(src, name):
-            raw = sb.tile([P, PACK, N], F32, name=name)
+            raw = shared.tile([P, PACK, N], F32, name=name, offset=WEIGHT_AT[name])
             nc.sync.dma_start(raw[:], src.rearrange("(p j) c -> p j c", j=PACK))
             return raw
 
@@ -61,31 +63,32 @@ def tile_picked_kqmedhopdhop_none_p_kernel(tc, x_words, x_scales, w1, w2, ga, gb
         def dealt_in(tile, h):
             return tile[:].rearrange("p k (m t) -> p m k t", t=PACK)[:, :, :, 2 * h : 2 * h + 2]
 
-        def product(lhs, rhs, t, tag):
-            acc = psum.tile([P, N], F32, name=tag)
+        def product(lhs, rhs, t, tag, moving=slice(0, N)):
+            acc = psum.tile([P, moving.stop - moving.start], F32, name=tag)
             cols = slice(t * P, (t + 1) * P)
             nc.tensor.matmul_mx(
                 out=acc[:],
                 lhsT=lhs[0][:, cols].bitcast(FP8X4),
                 lhsT_scale=lhs[1][:, cols],
-                rhs=rhs[0][:].bitcast(FP8X4),
-                rhs_scale=rhs[1][:],
+                rhs=rhs[0][:, moving].bitcast(FP8X4),
+                rhs_scale=rhs[1][:, moving],
                 start=True,
                 stop=True,
             )
             return acc
 
+        warm = sb.tile([P, 2], F32, name="warm")
+        nc.vector.memset(warm[:, 0:1], 0.0)
+        nc.scalar.activation(warm[:, 1:2], warm[:, 0:1], ACT.Sigmoid)
         table_scales = sb.tile([P, T], U8, name="table_scales")
-        nc.vector.memset(table_scales[:].bitcast(I32), 0)
         l_offs = load_list(offs, "l_offs")
-        w1_raw = load_weight(w1, "w1_raw")
         for q in range(4):
-            nc.sync.dma_start(
-                table_scales[32 * q : 32 * q + 4, :].bitcast(I32), x_scales[0, 4 * q : 4 * q + 4, :].bitcast(I32)
-            )
+            rows = x_scales[0, 4 * q : 4 * q + 4, :].bitcast(I32)
+            nc.sync.dma_start(table_scales[32 * q : 32 * q + 32, :].bitcast(I32), rows.partition_broadcast(8))
+        l_two = load_list(two, "l_two")
+        w1_raw = load_weight(w1, "w1_raw")
         table_words = sb.tile([P, T], I32, name="table_words")
         nc.sync.dma_start(table_words[:], x_words[0].rearrange("p n t -> p (n t)").bitcast(I32))
-        l_two = load_list(two, "l_two")
         ga_t = load_gain(ga, "ga_t")
         l1 = load_list(n1, "l1")
         l2 = load_list(n2, "l2")
@@ -100,25 +103,27 @@ def tile_picked_kqmedhopdhop_none_p_kernel(tc, x_words, x_scales, w1, w2, ga, gb
         xb = mx_pair("xb")
         w1q = mx_pair("w1q")
         w1_bf = [staged("w1_bf0"), staged("w1_bf1")]
-        for h in range(2):
-            nc.scalar.copy(dealt_out(w1_bf[h]), dealt_in(w1_raw, h))
         nc.vector.tensor_copy(xa[1][:], table_scales[:].indirect(l_offs[:]))
-        quantize(w1q, 0, w1_bf[0])
-        nc.vector.tensor_copy(xa[0][:], table_words[:].bitcast(U32).indirect(l_offs[:]))
-        quantize(w1q, 1, w1_bf[1])
         nc.vector.tensor_copy(xb[1][:], table_scales[:].indirect(l_two[:]))
+        nc.vector.tensor_copy(dealt_out(w1_bf[0]), dealt_in(w1_raw, 0))
+        nc.scalar.copy(dealt_out(w1_bf[1]), dealt_in(w1_raw, 1))
+        quantize(w1q, 0, w1_bf[0])
+        quantize(w1q, 1, w1_bf[1])
+        left, right = slice(0, HALF), slice(HALF, N)
+        for cols in (left, right):
+            places = l_offs[:, cols.start // 16 : cols.stop // 16]
+            nc.vector.tensor_copy(xa[0][:, cols], table_words[:].bitcast(U32).indirect(places))
         nc.vector.tensor_copy(xb[0][:], table_words[:].bitcast(U32).indirect(l_two[:]))
 
-        win_a = [sb.tile([P, WINDOW], F32, name=f"win_a{t}") for t in range(PACK)]
+        win_a = [shared.tile([P, WINDOW], F32, name=f"win_a{t}", offset=4096 * t) for t in range(PACK)]
         win_b = [sb.tile([P, WINDOW], F32, name=f"win_b{t}") for t in range(PACK)]
         a_plain = sb.tile([P, PACK, N], F32, name="a_plain")
         b_plain = sb.tile([P, PACK, N], F32, name="b_plain")
-        b_gain = sb.tile([P, PACK, N], F32, name="b_gain")
+        b_gain = sb.tile([P, PACK, N], F32, name="b_gain", align_bytes=64)
         d1 = sb.tile([P, PACK, N], F32, name="d1")
         d2 = sb.tile([P, PACK, N], F32, name="d2")
-        upper = sb.tile([P, PACK, N], F32, name="upper")
         mid = sb.tile([P, PACK, N], F32, name="mid")
-        gate = sb.tile([P, PACK, N], F32, name="gate")
+        gate = sb.tile([P, PACK, N], F32, name="gate", align_bytes=64)
         st = [sb.tile([P, N], F32, name=f"st{t}") for t in range(PACK)]
 
         def project_a(t):
@@ -132,19 +137,17 @@ def tile_picked_kqmedhopdhop_none_p_kernel(tc, x_words, x_scales, w1, w2, ga, gb
 
         def clip_above(h):
             rows = slice(2 * h, 2 * h + 2)
-            nc.vector.scalar_tensor_tensor(upper[:, rows, :], d1[:, rows, :], 0.0, d2[:, rows, :], ALU.max, ALU.min)
+            nc.vector.scalar_tensor_tensor(upper[h], d1[:, rows, :], 0.0, d2[:, rows, :], ALU.max, ALU.min)
 
         def clip_below(h):
             rows = slice(2 * h, 2 * h + 2)
-            nc.vector.scalar_tensor_tensor(mid[:, rows, :], d1[:, rows, :], 0.0, upper[:, rows, :], ALU.min, ALU.max)
-
-        b_acc = []
+            nc.vector.scalar_tensor_tensor(mid[:, rows, :], d1[:, rows, :], 0.0, upper[h], ALU.min, ALU.max)
 
         def project_b(t):
             acc = product(w2q, xb, t, f"bank_b{t}")
-            b_acc.append(acc)
             nc.scalar.copy(win_b[t][:, :N], acc[:])
             nc.scalar.copy(b_plain[:, t, :], acc[:])
+            nc.scalar.activation(b_gain[:, t, :], acc[:], ACT.Copy, scale=gb_t[:, t : t + 1])
 
         def step_b(t):
             nc.vector.tensor_tensor(st[t][:], win_b[t][:].indirect(l3[:]), b_plain[:, t, :], ALU.subtract)
@@ -156,9 +159,11 @@ def tile_picked_kqmedhopdhop_none_p_kernel(tc, x_words, x_scales, w1, w2, ga, gb
                     st[t][:].indirect(l4[:, h * HALF // 16 : (h + 1) * HALF // 16]),
                     ACT.Sigmoid,
                 )
-            nc.scalar.activation(b_gain[:, t, :], b_acc[t][:], ACT.Copy, scale=gb_t[:, t : t + 1])
 
-        project_a(0)
+        for cols, bank in ((left, "bank_a0"), (right, "bank_b0")):
+            acc = product(w1q, xa, 0, bank, cols)
+            nc.scalar.activation(win_a[0][:, cols], acc[:], ACT.Copy, scale=ga_t[:, 0:1])
+            nc.scalar.activation(a_plain[:, 0, cols], acc[:], ACT.Copy, scale=ga_t[:, 0:1])
         project_a(1)
         w2q = mx_pair("w2q")
         w2_bf = [staged("w2_bf0"), staged("w2_bf1")]
@@ -170,6 +175,8 @@ def tile_picked_kqmedhopdhop_none_p_kernel(tc, x_words, x_scales, w1, w2, ga, gb
         project_a(3)
         for h in range(2):
             quantize(w2q, h, w2_bf[h])
+        upper0 = sb.tile([P, 2, N], F32, name="w2_bf1", align_bytes=64)
+        upper = [upper0[:], b_plain[:, 2:4, :]]
         clip_above(0)
         project_b(0)
         project_b(1)
@@ -191,34 +198,48 @@ def tile_picked_kqmedhopdhop_none_p_kernel(tc, x_words, x_scales, w1, w2, ga, gb
 
         zq = mx_pair("zq")
         z2q = mx_pair("z2q")
-        z_bf = [staged("z_bf0"), staged("z_bf1")]
         z2_bf = [staged("z2_bf0"), staged("z2_bf1")]
 
         def finish_z2(h):
             cols = slice(h * HALF, (h + 1) * HALF)
             nc.vector.tensor_tensor(
-                z2_bf[h][:].rearrange("p (c i k) -> p c k i", i=4, k=PACK),
-                b_gain[:, :, cols].rearrange("p k (c i) -> p c k i", i=4),
-                gate[:, :, cols].rearrange("p k (c i) -> p c k i", i=4),
+                z2_bf[h][:].rearrange("p (c i k) -> p c k i", i=2, k=PACK),
+                b_gain[:, :, cols].rearrange("p k (c i) -> p c k i", i=2),
+                gate[:, :, cols].rearrange("p k (c i) -> p c k i", i=2),
                 ALU.mult,
             )
 
-        def finish_z(h):
-            nc.vector.tensor_tensor(dealt_out(z_bf[h]), dealt_in(mid, h), dealt_in(a_plain, h), ALU.add)
+        def finish_z(t):
+            nc.vector.tensor_tensor(
+                z_bf[t].rearrange("p (m i k) -> p m k i", i=2, k=PACK),
+                mid[:].rearrange("p k (m t i) -> p t m k i", t=PACK, i=2)[:, t],
+                a_plain[:].rearrange("p k (m t i) -> p t m k i", t=PACK, i=2)[:, t],
+                ALU.add,
+            )
+
+        def quantize_z(t):
+            cols = slice(t * P, (t + 1) * P)
+            nc.vector.quantize_mx(out=zq[0][:, cols].bitcast(FP8X4), scales=zq[1][:, cols], in_=z_bf[t])
 
         finish_z2(0)
         finish_z2(1)
+        z_pairs = [staged("gate"), staged("b_gain")]
+        z_bf = [z_pairs[t // 2][:, (t % 2) * N : (t % 2 + 1) * N] for t in range(PACK)]
         quantize(z2q, 0, z2_bf[0])
         finish_z(0)
         quantize(z2q, 1, z2_bf[1])
-        quantize(zq, 0, z_bf[0])
+        quantize_z(0)
         finish_z(1)
-        quantize(zq, 1, z_bf[1])
+        finish_z(2)
+        quantize_z(1)
+        finish_z(3)
+        quantize_z(2)
+        quantize_z(3)
 
         s_plain = [sb.tile([P, N], F32, name=f"s_plain{t}") for t in range(PACK)]
         st2_plain = [sb.tile([P, N], F32, name=f"st2_plain{t}") for t in range(PACK)]
         result = [sb.tile([P, N], F32, name=f"result{t}") for t in range(PACK)]
-        out_rows = out.rearrange("(p t) v -> p t v", t=PACK)
+        out_rows = out.rearrange("(m t i) v -> t m i v", t=PACK, i=2)
 
         def scores(t):
             acc = product(zq, z2q, t, f"bank_a{t}")
@@ -229,9 +250,10 @@ def tile_picked_kqmedhopdhop_none_p_kernel(tc, x_words, x_scales, w1, w2, ga, gb
             nc.vector.tensor_tensor(win_b[t][:, :N], win_a[t][:].indirect(l5[:]), s_plain[t][:], ALU.add)
             nc.scalar.copy(st2_plain[t][:], win_b[t][:, :N])
 
-        def second_hop(t):
-            nc.vector.tensor_tensor(result[t][:], win_b[t][:].indirect(l6[:]), st2_plain[t][:], ALU.subtract)
-            nc.sync.dma_start(out_rows[:, t, :], result[t][:])
+        def second_hop(t, cols=slice(0, N)):
+            places = l6[:, cols.start // 16 : cols.stop // 16]
+            nc.vector.tensor_tensor(result[t][:, cols], win_b[t][:].indirect(places), st2_plain[t][:, cols], ALU.subtract)
+            nc.sync.dma_start(out_rows[t, :, :, cols], result[t][:, cols])
 
         scores(0)
         scores(1)
@@ -244,4 +266,5 @@ def tile_picked_kqmedhopdhop_none_p_kernel(tc, x_words, x_scales, w1, w2, ga, gb
         second_hop(1)
         first_hop(3)
         second_hop(2)
-        second_hop(3)
+        second_hop(3, left)
+        second_hop(3, right)

@@ -1,6 +1,7 @@
 from contextlib import ExitStack
 
 import concourse.mybir as mybir
+from concourse.masks import make_identity
 
 K, T, S, V, H = 512, 2048, 512, 512, 512
 FLOPS = 2 * K * H * S + 2 * K * H * V + 2 * H * S * V
@@ -80,6 +81,8 @@ def tile_picked_kqmedhopdhop_none_p_kernel(tc, x_words, x_scales, w1, w2, ga, gb
         warm = sb.tile([P, 2], F32, name="warm")
         nc.vector.memset(warm[:, 0:1], 0.0)
         nc.scalar.activation(warm[:, 1:2], warm[:, 0:1], ACT.Sigmoid)
+        ident = sb.tile([P, P], F32, name="ident")
+        make_identity(nc, ident[:])
         table_scales = sb.tile([P, T], U8, name="table_scales")
         l_offs = load_list(offs, "l_offs")
         for q in range(4):
@@ -118,41 +121,40 @@ def tile_picked_kqmedhopdhop_none_p_kernel(tc, x_words, x_scales, w1, w2, ga, gb
         win_a = [shared.tile([P, WINDOW], F32, name=f"win_a{t}", offset=4096 * t) for t in range(PACK)]
         win_b = [sb.tile([P, WINDOW], F32, name=f"win_b{t}") for t in range(PACK)]
         a_plain = sb.tile([P, PACK, N], F32, name="a_plain")
-        b_plain = sb.tile([P, PACK, N], F32, name="b_plain")
+        b_plain = [sb.tile([P, N], F32, name=f"b_plain{t}", align_bytes=64) for t in range(PACK)]
         b_gain = sb.tile([P, PACK, N], F32, name="b_gain", align_bytes=64)
         d1 = sb.tile([P, PACK, N], F32, name="d1")
         d2 = sb.tile([P, PACK, N], F32, name="d2")
-        mid = sb.tile([P, PACK, N], F32, name="mid")
         gate = sb.tile([P, PACK, N], F32, name="gate", align_bytes=64)
         st = [sb.tile([P, N], F32, name=f"st{t}") for t in range(PACK)]
 
         def project_a(t):
             acc = product(w1q, xa, t, f"bank_a{t}")
             nc.scalar.activation(win_a[t][:, :N], acc[:], ACT.Copy, scale=ga_t[:, t : t + 1])
-            nc.scalar.activation(a_plain[:, t, :], acc[:], ACT.Copy, scale=ga_t[:, t : t + 1])
+            if t < 2:
+                nc.scalar.activation(a_plain[:, t, :], acc[:], ACT.Copy, scale=ga_t[:, t : t + 1])
+            else:
+                nc.sync.dma_start(a_plain[:, t, :], win_a[t][:, :N])
 
-        def pulls(t):
-            nc.vector.tensor_tensor(d1[:, t, :], win_a[t][:].indirect(l1[:]), a_plain[:, t, :], ALU.subtract)
-            nc.vector.tensor_tensor(d2[:, t, :], win_a[t][:].indirect(l2[:]), a_plain[:, t, :], ALU.subtract)
+        def pull(dst, places, t):
+            nc.vector.tensor_tensor(dst[:, t, :], win_a[t][:].indirect(places[:]), a_plain[:, t, :], ALU.subtract)
 
-        def clip_above(h):
+        def clip_above(h, upper):
             rows = slice(2 * h, 2 * h + 2)
-            nc.vector.scalar_tensor_tensor(upper[h], d1[:, rows, :], 0.0, d2[:, rows, :], ALU.max, ALU.min)
+            nc.vector.scalar_tensor_tensor(upper[:], d1[:, rows, :], 0.0, d2[:, rows, :], ALU.max, ALU.min)
 
-        def clip_below(h):
+        def clip_below(h, upper):
             rows = slice(2 * h, 2 * h + 2)
-            nc.vector.scalar_tensor_tensor(mid[:, rows, :], d1[:, rows, :], 0.0, upper[h], ALU.min, ALU.max)
+            nc.vector.scalar_tensor_tensor(mid[:, rows, :], d1[:, rows, :], 0.0, upper[:], ALU.min, ALU.max)
 
         def project_b(t):
-            acc = product(w2q, xb, t, f"bank_b{t}")
+            acc = product(w2q, xb, t, ("bank_a2", "bank_a3", "bank_b2", "bank_b3")[t])
             nc.scalar.copy(win_b[t][:, :N], acc[:])
-            nc.scalar.copy(b_plain[:, t, :], acc[:])
+            nc.sync.dma_start(b_plain[t][:], win_b[t][:, :N])
             nc.scalar.activation(b_gain[:, t, :], acc[:], ACT.Copy, scale=gb_t[:, t : t + 1])
 
         def step_b(t):
-            nc.vector.tensor_tensor(st[t][:], win_b[t][:].indirect(l3[:]), b_plain[:, t, :], ALU.subtract)
-
-        def gate_b(t):
+            nc.vector.tensor_tensor(st[t][:], win_b[t][:].indirect(l3[:]), b_plain[t][:], ALU.subtract)
             for h in range(2):
                 nc.scalar.activation(
                     gate[:, t, h * HALF : (h + 1) * HALF],
@@ -169,41 +171,57 @@ def tile_picked_kqmedhopdhop_none_p_kernel(tc, x_words, x_scales, w1, w2, ga, gb
         w2_bf = [staged("w2_bf0"), staged("w2_bf1")]
         for h in range(2):
             nc.scalar.copy(dealt_out(w2_bf[h]), dealt_in(w2_raw, h))
-        pulls(0)
-        pulls(1)
         project_a(2)
         project_a(3)
+        for t in (0, 1):
+            pull(d1, l1, t)
+            pull(d2, l2, t)
+        upper = sb.tile([P, 2, N], F32, name="upper")
+        clip_above(0, upper)
         for h in range(2):
             quantize(w2q, h, w2_bf[h])
-        upper0 = sb.tile([P, 2, N], F32, name="w2_bf1", align_bytes=64)
-        upper = [upper0[:], b_plain[:, 2:4, :]]
-        clip_above(0)
-        project_b(0)
-        project_b(1)
-        pulls(2)
-        clip_below(0)
+        mid = sb.tile([P, PACK, N], F32, name="w2_bf1", align_bytes=64)
+        clip_below(0, upper)
+        turned = {t: psum.tile([P, PACK, P], F32, name=f"bank_b{t - 2}") for t in (2, 3)}
+
+        def turn(t, src, k, start=False, stop=False):
+            columns = src[:, k, :].rearrange("p (m t) -> p t m", t=PACK)[:, t, :]
+            nc.tensor.matmul(turned[t][:, k, :], columns, ident[:], start=start, stop=stop, is_transpose=True)
+
+        for t in range(PACK):
+            project_b(t)
+        for t in (2, 3):
+            pull(d1, l1, t)
+            pull(d2, l2, t)
+        for t in (2, 3):
+            for k in range(PACK):
+                turn(t, a_plain, k, start=(k == 0))
+            for k in (0, 1):
+                turn(t, mid, k)
         step_b(0)
+        upper = sb.tile([P, 2, N], F32, name="b_plain0", align_bytes=64)
+        clip_above(1, upper)
         step_b(1)
-        project_b(2)
-        project_b(3)
-        gate_b(0)
-        gate_b(1)
-        pulls(3)
+        clip_below(1, upper)
         step_b(2)
         step_b(3)
-        gate_b(2)
-        gate_b(3)
-        clip_above(1)
-        clip_below(1)
 
         zq = mx_pair("zq")
         z2q = mx_pair("z2q")
-        z2_bf = [staged("z2_bf0"), staged("z2_bf1")]
+        pieces = [slice(0, HALF), slice(HALF, HALF + P), slice(HALF + P, N)]
+        z2_bf = [
+            sb.tile([P, PACK * (cols.stop - cols.start)], BF16, name=f"z2_bf{n}", align_bytes=64)
+            for n, cols in enumerate(pieces)
+        ]
 
-        def finish_z2(h):
-            cols = slice(h * HALF, (h + 1) * HALF)
+        def quantize_z2(n):
+            cols = pieces[n]
+            nc.vector.quantize_mx(out=z2q[0][:, cols].bitcast(FP8X4), scales=z2q[1][:, cols], in_=z2_bf[n][:])
+
+        def finish_z2(n):
+            cols = pieces[n]
             nc.vector.tensor_tensor(
-                z2_bf[h][:].rearrange("p (c i k) -> p c k i", i=2, k=PACK),
+                z2_bf[n][:].rearrange("p (c i k) -> p c k i", i=2, k=PACK),
                 b_gain[:, :, cols].rearrange("p k (c i) -> p c k i", i=2),
                 gate[:, :, cols].rearrange("p k (c i) -> p c k i", i=2),
                 ALU.mult,
@@ -211,40 +229,59 @@ def tile_picked_kqmedhopdhop_none_p_kernel(tc, x_words, x_scales, w1, w2, ga, gb
 
         def finish_z(t):
             nc.vector.tensor_tensor(
-                z_bf[t].rearrange("p (m i k) -> p m k i", i=2, k=PACK),
-                mid[:].rearrange("p k (m t i) -> p t m k i", t=PACK, i=2)[:, t],
-                a_plain[:].rearrange("p k (m t i) -> p t m k i", t=PACK, i=2)[:, t],
+                z_bf[t][:].rearrange("p (m i k) -> p m k i", i=2, k=PACK),
+                mid[:].rearrange("p k (m g r) -> p g m k r", g=2, r=PACK)[:, t, :, :, 0:2],
+                a_plain[:].rearrange("p k (m g r) -> p g m k r", g=2, r=PACK)[:, t, :, :, 0:2],
                 ALU.add,
+            )
+
+        def turn_back(t):
+            turn(t, mid, 2)
+            turn(t, mid, 3, stop=True)
+            by_place = sb.tile([P, N], BF16, name=f"by_place{t}")
+            nc.scalar.copy(
+                by_place[:].rearrange("j (u p e) -> j u p e", u=2, e=2),
+                turned[t][:].rearrange("j (u e) p -> j u p e", u=2),
+            )
+            back = psum.tile([P, 2, P], F32, name=f"bank_b{t}")
+            for u in range(2):
+                nc.tensor.transpose(back[:, u, :], by_place[:].bitcast(F32)[:, u * P : (u + 1) * P], ident[:])
+            nc.scalar.copy(
+                z_bf[t][:].bitcast(F32).rearrange("p (m u) -> p m u", u=2), back[:].rearrange("p u m -> p m u")
             )
 
         def quantize_z(t):
             cols = slice(t * P, (t + 1) * P)
-            nc.vector.quantize_mx(out=zq[0][:, cols].bitcast(FP8X4), scales=zq[1][:, cols], in_=z_bf[t])
+            nc.vector.quantize_mx(out=zq[0][:, cols].bitcast(FP8X4), scales=zq[1][:, cols], in_=z_bf[t][:])
 
-        finish_z2(0)
-        finish_z2(1)
-        z_pairs = [staged("gate"), staged("b_gain")]
-        z_bf = [z_pairs[t // 2][:, (t % 2) * N : (t % 2 + 1) * N] for t in range(PACK)]
-        quantize(z2q, 0, z2_bf[0])
+        z_bf = {t: sb.tile([P, N], BF16, name=f"z_bf{t}", align_bytes=64) for t in (2, 3)}
+        z_bf[0] = sb.tile([P, N], BF16, name="b_plain3", align_bytes=64)
+        turn_back(2)
+        turn_back(3)
         finish_z(0)
-        quantize(z2q, 1, z2_bf[1])
+        finish_z2(0)
         quantize_z(0)
+        quantize_z2(0)
+        finish_z2(1)
+        finish_z2(2)
+        quantize_z2(1)
+        quantize_z2(2)
+        z_bf[1] = sb.tile([P, N], BF16, name="gate", align_bytes=64)
         finish_z(1)
-        finish_z(2)
-        quantize_z(1)
-        finish_z(3)
         quantize_z(2)
         quantize_z(3)
+        quantize_z(1)
 
         s_plain = [sb.tile([P, N], F32, name=f"s_plain{t}") for t in range(PACK)]
         st2_plain = [sb.tile([P, N], F32, name=f"st2_plain{t}") for t in range(PACK)]
         result = [sb.tile([P, N], F32, name=f"result{t}") for t in range(PACK)]
-        out_rows = out.rearrange("(m t i) v -> t m i v", t=PACK, i=2)
+        rows_in_pairs = out.rearrange("(m g r) v -> g m r v", g=2, r=PACK)
+        rows_single = out.rearrange("(m t) v -> t m v", t=PACK)
 
-        def scores(t):
-            acc = product(zq, z2q, t, f"bank_a{t}")
-            nc.scalar.activation(win_a[t][:, :N], acc[:], ACT.Copy, scale=-0.03125)
-            nc.scalar.activation(s_plain[t][:], acc[:], ACT.Copy, scale=-0.0625)
+        def scores(t, bank, cols=slice(0, N)):
+            acc = product(zq, z2q, t, bank, cols)
+            nc.scalar.activation(win_a[t][:, cols], acc[:], ACT.Copy, scale=-0.03125)
+            nc.scalar.activation(s_plain[t][:, cols], acc[:], ACT.Copy, scale=-0.0625)
 
         def first_hop(t):
             nc.vector.tensor_tensor(win_b[t][:, :N], win_a[t][:].indirect(l5[:]), s_plain[t][:], ALU.add)
@@ -253,18 +290,20 @@ def tile_picked_kqmedhopdhop_none_p_kernel(tc, x_words, x_scales, w1, w2, ga, gb
         def second_hop(t, cols=slice(0, N)):
             places = l6[:, cols.start // 16 : cols.stop // 16]
             nc.vector.tensor_tensor(result[t][:, cols], win_b[t][:].indirect(places), st2_plain[t][:, cols], ALU.subtract)
-            nc.sync.dma_start(out_rows[t, :, :, cols], result[t][:, cols])
+            rows = rows_in_pairs[t, :, 0:2, cols] if t < 2 else rows_single[t, :, cols]
+            nc.sync.dma_start(rows, result[t][:, cols])
 
-        scores(0)
-        scores(1)
+        for cols, bank in zip(pieces, ("bank_a0", "bank_a1", "bank_a3")):
+            scores(0, bank, cols)
+        scores(2, "bank_a2")
         first_hop(0)
-        scores(2)
-        first_hop(1)
-        scores(3)
-        second_hop(0)
+        scores(3, "bank_a0")
         first_hop(2)
-        second_hop(1)
+        scores(1, "bank_a1")
+        second_hop(0)
         first_hop(3)
         second_hop(2)
-        second_hop(3, left)
-        second_hop(3, right)
+        first_hop(1)
+        second_hop(3)
+        second_hop(1, left)
+        second_hop(1, right)

@@ -78,9 +78,6 @@ def tile_picked_kqmedhopdhop_none_p_kernel(tc, x_words, x_scales, w1, w2, ga, gb
             )
             return acc
 
-        warm = sb.tile([P, 2], F32, name="warm")
-        nc.vector.memset(warm[:, 0:1], 0.0)
-        nc.scalar.activation(warm[:, 1:2], warm[:, 0:1], ACT.Sigmoid)
         ident = sb.tile([P, P], F32, name="ident")
         make_identity(nc, ident[:])
         table_scales = sb.tile([P, T], U8, name="table_scales")
@@ -131,7 +128,7 @@ def tile_picked_kqmedhopdhop_none_p_kernel(tc, x_words, x_scales, w1, w2, ga, gb
         def project_a(t):
             acc = product(w1q, xa, t, f"bank_a{t}")
             nc.scalar.activation(win_a[t][:, :N], acc[:], ACT.Copy, scale=ga_t[:, t : t + 1])
-            if t < 2:
+            if t < 3:
                 nc.scalar.activation(a_plain[:, t, :], acc[:], ACT.Copy, scale=ga_t[:, t : t + 1])
             else:
                 nc.sync.dma_start(a_plain[:, t, :], win_a[t][:, :N])

from contextlib import ExitStack

import concourse.mybir as mybir
from concourse.masks import make_identity

K, T, S, V, H = 512, 2048, 512, 512, 512
FLOPS = 2 * K * H * S + 2 * K * H * V + 2 * H * S * V

F32 = mybir.dt.float32
BF16 = mybir.dt.bfloat16
I32 = mybir.dt.int32
U32 = mybir.dt.uint32
U16 = mybir.dt.uint16
U8 = mybir.dt.uint8
FP8X4 = mybir.dt.float8_e4m3fn_x4
ALU = mybir.AluOpType
ACT = mybir.ActivationFunctionType

P = 128
PACK = 4
N = 512
HALF = N // 2
WINDOW = 2 * N
WEIGHT_AT = {"w1_raw": 0, "w2_raw": 8192}


def tile_picked_kqmedhopdhop_none_p_kernel(tc, x_words, x_scales, w1, w2, ga, gb, offs, two, n1, n2, n3, n4, n5, n6, out):
    nc = tc.nc
    with ExitStack() as ctx:
        sb = ctx.enter_context(tc.tile_pool(name="sb", bufs=1))
        shared = ctx.enter_context(tc.tile_pool(name="shared", bufs=1))
        psum = ctx.enter_context(tc.psum_pool(name="psum", bufs=1))

        def load_list(src, name):
            tile = sb.tile([P, N // 16], U16, name=name)
            nc.sync.dma_start(tile[:], src)
            return tile

        def load_weight(src, name):
            raw = shared.tile([P, PACK, N], F32, name=name, offset=WEIGHT_AT[name])
            nc.sync.dma_start(raw[:], src.rearrange("(p j) c -> p j c", j=PACK))
            return raw

        def load_gain(src, name):
            tile = sb.tile([P, PACK], F32, name=name)
            nc.sync.dma_start(tile[:], src.rearrange("(p t) o -> p (t o)", t=PACK))
            return tile

        def mx_pair(name):
            codes = sb.tile([P, N], U32, name=name + "_codes", align_bytes=64)
            scales = sb.tile([P, N], U8, name=name + "_scales", align_bytes=64)
            return codes, scales

        def staged(name):
            return sb.tile([P, PACK * HALF], BF16, name=name, align_bytes=64)

        def quantize(pair, h, src):
            cols = slice(h * HALF, (h + 1) * HALF)
            nc.vector.quantize_mx(out=pair[0][:, cols].bitcast(FP8X4), scales=pair[1][:, cols], in_=src[:])

        def dealt_out(tile):
            return tile[:].rearrange("p (e m k) -> p m k e", e=2, k=PACK)

        def dealt_in(tile, h):
            return tile[:].rearrange("p k (m t) -> p m k t", t=PACK)[:, :, :, 2 * h : 2 * h + 2]

        def product(lhs, rhs, t, tag, moving=slice(0, N)):
            acc = psum.tile([P, moving.stop - moving.start], F32, name=tag)
            cols = slice(t * P, (t + 1) * P)
            nc.tensor.matmul_mx(
                out=acc[:],
                lhsT=lhs[0][:, cols].bitcast(FP8X4),
                lhsT_scale=lhs[1][:, cols],
                rhs=rhs[0][:, moving].bitcast(FP8X4),
                rhs_scale=rhs[1][:, moving],
                start=True,
                stop=True,
            )
            return acc

        ident = sb.tile([P, P], F32, name="ident")
        make_identity(nc, ident[:])
        table_scales = sb.tile([P, T], U8, name="table_scales")
        l_offs = load_list(offs, "l_offs")
        for q in range(4):
            rows = x_scales[0, 4 * q : 4 * q + 4, :].bitcast(I32)
            nc.sync.dma_start(table_scales[32 * q : 32 * q + 32, :].bitcast(I32), rows.partition_broadcast(8))
        l_two = load_list(two, "l_two")
        w1_raw = load_weight(w1, "w1_raw")
        table_words = sb.tile([P, T], I32, name="table_words")
        nc.sync.dma_start(table_words[:], x_words[0].rearrange("p n t -> p (n t)").bitcast(I32))
        ga_t = load_gain(ga, "ga_t")
        l1 = load_list(n1, "l1")
        l2 = load_list(n2, "l2")
        w2_raw = load_weight(w2, "w2_raw")
        gb_t = load_gain(gb, "gb_t")
        l3 = load_list(n3, "l3")
        l4 = load_list(n4, "l4")
        l5 = load_list(n5, "l5")
        l6 = load_list(n6, "l6")

        xa = mx_pair("xa")
        xb = mx_pair("xb")
        w1q = mx_pair("w1q")
        w1_bf = [staged("w1_bf0"), staged("w1_bf1")]
        nc.vector.tensor_copy(xa[1][:], table_scales[:].indirect(l_offs[:]))
        nc.vector.tensor_copy(xb[1][:], table_scales[:].indirect(l_two[:]))
        nc.vector.tensor_copy(dealt_out(w1_bf[0]), dealt_in(w1_raw, 0))
        nc.scalar.copy(dealt_out(w1_bf[1]), dealt_in(w1_raw, 1))
        quantize(w1q, 0, w1_bf[0])
        quantize(w1q, 1, w1_bf[1])
        left, right = slice(0, HALF), slice(HALF, N)
        for cols in (left, right):
            places = l_offs[:, cols.start // 16 : cols.stop // 16]
            nc.vector.tensor_copy(xa[0][:, cols], table_words[:].bitcast(U32).indirect(places))
        nc.vector.tensor_copy(xb[0][:], table_words[:].bitcast(U32).indirect(l_two[:]))

        win_a = [shared.tile([P, WINDOW], F32, name=f"win_a{t}", offset=4096 * t) for t in range(PACK)]
        win_b = [sb.tile([P, WINDOW], F32, name=f"win_b{t}") for t in range(PACK)]
        a_plain = sb.tile([P, PACK, N], F32, name="a_plain")
        b_plain = [sb.tile([P, N], F32, name=f"b_plain{t}", align_bytes=64) for t in range(PACK)]
        b_gain = sb.tile([P, PACK, N], F32, name="b_gain", align_bytes=64)
        d1 = sb.tile([P, PACK, N], F32, name="d1")
        d2 = sb.tile([P, PACK, N], F32, name="d2")
        gate = sb.tile([P, PACK, N], F32, name="gate", align_bytes=64)
        st = [sb.tile([P, N], F32, name=f"st{t}") for t in range(PACK)]

        def project_a(t):
            acc = product(w1q, xa, t, f"bank_a{t}")
            nc.scalar.activation(win_a[t][:, :N], acc[:], ACT.Copy, scale=ga_t[:, t : t + 1])
            if t < 3:
                nc.scalar.activation(a_plain[:, t, :], acc[:], ACT.Copy, scale=ga_t[:, t : t + 1])
            else:
                nc.sync.dma_start(a_plain[:, t, :], win_a[t][:, :N])

        def pull(dst, places, t):
            nc.vector.tensor_tensor(dst[:, t, :], win_a[t][:].indirect(places[:]), a_plain[:, t, :], ALU.subtract)

        def clip_above(h, upper):
            rows = slice(2 * h, 2 * h + 2)
            nc.vector.scalar_tensor_tensor(upper[:], d1[:, rows, :], 0.0, d2[:, rows, :], ALU.max, ALU.min)

        def clip_below(h, upper):
            rows = slice(2 * h, 2 * h + 2)
            nc.vector.scalar_tensor_tensor(mid[:, rows, :], d1[:, rows, :], 0.0, upper[:], ALU.min, ALU.max)

        def project_b(t):
            acc = product(w2q, xb, t, ("bank_a2", "bank_a3", "bank_b2", "bank_b3")[t])
            nc.scalar.copy(win_b[t][:, :N], acc[:])
            nc.sync.dma_start(b_plain[t][:], win_b[t][:, :N])
            nc.scalar.activation(b_gain[:, t, :], acc[:], ACT.Copy, scale=gb_t[:, t : t + 1])

        def step_b(t):
            nc.vector.tensor_tensor(st[t][:], win_b[t][:].indirect(l3[:]), b_plain[t][:], ALU.subtract)
            for h in range(2):
                nc.scalar.activation(
                    gate[:, t, h * HALF : (h + 1) * HALF],
                    st[t][:].indirect(l4[:, h * HALF // 16 : (h + 1) * HALF // 16]),
                    ACT.Sigmoid,
                )

        for cols, bank in ((left, "bank_a0"), (right, "bank_b0")):
            acc = product(w1q, xa, 0, bank, cols)
            nc.scalar.activation(win_a[0][:, cols], acc[:], ACT.Copy, scale=ga_t[:, 0:1])
            nc.scalar.activation(a_plain[:, 0, cols], acc[:], ACT.Copy, scale=ga_t[:, 0:1])
        project_a(1)
        w2q = mx_pair("w2q")
        w2_bf = [staged("w2_bf0"), staged("w2_bf1")]
        for h in range(2):
            nc.scalar.copy(dealt_out(w2_bf[h]), dealt_in(w2_raw, h))
        project_a(2)
        project_a(3)
        for t in (0, 1):
            pull(d1, l1, t)
            pull(d2, l2, t)
        upper = sb.tile([P, 2, N], F32, name="upper")
        clip_above(0, upper)
        for h in range(2):
            quantize(w2q, h, w2_bf[h])
        mid = sb.tile([P, PACK, N], F32, name="w2_bf1", align_bytes=64)
        clip_below(0, upper)
        turned = {t: psum.tile([P, PACK, P], F32, name=f"bank_b{t - 2}") for t in (2, 3)}

        def turn(t, src, k, start=False, stop=False):
            columns = src[:, k, :].rearrange("p (m t) -> p t m", t=PACK)[:, t, :]
            nc.tensor.matmul(turned[t][:, k, :], columns, ident[:], start=start, stop=stop, is_transpose=True)

        for t in range(PACK):
            project_b(t)
        for t in (2, 3):
            pull(d1, l1, t)
            pull(d2, l2, t)
        for t in (2, 3):
            for k in range(PACK):
                turn(t, a_plain, k, start=(k == 0))
            for k in (0, 1):
                turn(t, mid, k)
        step_b(0)
        upper = sb.tile([P, 2, N], F32, name="b_plain0", align_bytes=64)
        clip_above(1, upper)
        step_b(1)
        clip_below(1, upper)
        step_b(2)
        step_b(3)

        zq = mx_pair("zq")
        z2q = mx_pair("z2q")
        pieces = [slice(0, HALF), slice(HALF, HALF + P), slice(HALF + P, N)]
        z2_bf = [
            sb.tile([P, PACK * (cols.stop - cols.start)], BF16, name=f"z2_bf{n}", align_bytes=64)
            for n, cols in enumerate(pieces)
        ]

        def quantize_z2(n):
            cols = pieces[n]
            nc.vector.quantize_mx(out=z2q[0][:, cols].bitcast(FP8X4), scales=z2q[1][:, cols], in_=z2_bf[n][:])

        def finish_z2(n):
            cols = pieces[n]
            nc.vector.tensor_tensor(
                z2_bf[n][:].rearrange("p (c i k) -> p c k i", i=2, k=PACK),
                b_gain[:, :, cols].rearrange("p k (c i) -> p c k i", i=2),
                gate[:, :, cols].rearrange("p k (c i) -> p c k i", i=2),
                ALU.mult,
            )

        def finish_z(t):
            nc.vector.tensor_tensor(
                z_bf[t][:].rearrange("p (m i k) -> p m k i", i=2, k=PACK),
                mid[:].rearrange("p k (m g r) -> p g m k r", g=2, r=PACK)[:, t, :, :, 0:2],
                a_plain[:].rearrange("p k (m g r) -> p g m k r", g=2, r=PACK)[:, t, :, :, 0:2],
                ALU.add,
            )

        def turn_back(t):
            turn(t, mid, 2)
            turn(t, mid, 3, stop=True)
            by_place = sb.tile([P, N], BF16, name=f"by_place{t}")
            nc.scalar.copy(
                by_place[:].rearrange("j (u p e) -> j u p e", u=2, e=2),
                turned[t][:].rearrange("j (u e) p -> j u p e", u=2),
            )
            back = psum.tile([P, 2, P], F32, name=f"bank_b{t}")
            for u in range(2):
                nc.tensor.transpose(back[:, u, :], by_place[:].bitcast(F32)[:, u * P : (u + 1) * P], ident[:])
            nc.scalar.copy(
                z_bf[t][:].bitcast(F32).rearrange("p (m u) -> p m u", u=2), back[:].rearrange("p u m -> p m u")
            )

        def quantize_z(t):
            cols = slice(t * P, (t + 1) * P)
            nc.vector.quantize_mx(out=zq[0][:, cols].bitcast(FP8X4), scales=zq[1][:, cols], in_=z_bf[t][:])

        z_bf = {t: sb.tile([P, N], BF16, name=f"z_bf{t}", align_bytes=64) for t in (2, 3)}
        z_bf[0] = sb.tile([P, N], BF16, name="b_plain3", align_bytes=64)
        turn_back(2)
        turn_back(3)
        finish_z(0)
        finish_z2(0)
        quantize_z(0)
        quantize_z2(0)
        finish_z2(1)
        finish_z2(2)
        quantize_z2(1)
        quantize_z2(2)
        z_bf[1] = sb.tile([P, N], BF16, name="gate", align_bytes=64)
        finish_z(1)
        quantize_z(2)
        quantize_z(3)
        quantize_z(1)

        s_plain = [sb.tile([P, N], F32, name=f"s_plain{t}") for t in range(PACK)]
        st2_plain = [sb.tile([P, N], F32, name=f"st2_plain{t}") for t in range(PACK)]
        result = [sb.tile([P, N], F32, name=f"result{t}") for t in range(PACK)]
        rows_in_pairs = out.rearrange("(m g r) v -> g m r v", g=2, r=PACK)
        rows_single = out.rearrange("(m t) v -> t m v", t=PACK)

        def scores(t, bank, cols=slice(0, N)):
            acc = product(zq, z2q, t, bank, cols)
            nc.scalar.activation(win_a[t][:, cols], acc[:], ACT.Copy, scale=-0.03125)
            nc.scalar.activation(s_plain[t][:, cols], acc[:], ACT.Copy, scale=-0.0625)

        def first_hop(t):
            nc.vector.tensor_tensor(win_b[t][:, :N], win_a[t][:].indirect(l5[:]), s_plain[t][:], ALU.add)
            nc.scalar.copy(st2_plain[t][:], win_b[t][:, :N])

        def second_hop(t, cols=slice(0, N)):
            places = l6[:, cols.start // 16 : cols.stop // 16]
            nc.vector.tensor_tensor(result[t][:, cols], win_b[t][:].indirect(places), st2_plain[t][:, cols], ALU.subtract)
            rows = rows_in_pairs[t, :, 0:2, cols] if t < 2 else rows_single[t, :, cols]
            nc.sync.dma_start(rows, result[t][:, cols])

        for cols, bank in zip(pieces, ("bank_a0", "bank_a1", "bank_a3")):
            scores(0, bank, cols)
        scores(2, "bank_a2")
        first_hop(0)
        scores(3, "bank_a0")
        first_hop(2)
        scores(1, "bank_a1")
        second_hop(0)
        first_hop(3)
        second_hop(2)
        first_hop(1)
        second_hop(3)
        second_hop(1, left)
        second_hop(1, right)
